import numpy as np
import ml_dtypes


def mxq(x, axis, fmt="e4m3"):
    dtype, down = {"e4m3": (ml_dtypes.float8_e4m3fn, 7), "e5m2": (ml_dtypes.float8_e5m2, 14)}[fmt]
    v = np.moveaxis(np.asarray(x, np.float32).astype(ml_dtypes.bfloat16).astype(np.float64), axis, -1)
    blocks = v.reshape(v.shape[:-1] + (-1, 32))
    amax = np.abs(blocks).max(-1, keepdims=True)
    byte = np.maximum(np.where(amax > 0, np.frexp(amax)[1] - 1 + 127, 0) - down, 1)
    scale = np.exp2(byte - 127.0)
    codes = (blocks / scale).astype(np.float32).astype(dtype).astype(np.float64)
    return np.moveaxis((codes * scale).reshape(v.shape), -1, axis)


WIDE = False


def mx_kscale(k):
    if not WIDE:
        return np.ones(k)
    levels = np.array([10, -10, 5, -5, 0])
    if k % 512:
        return np.exp2(np.random.permutation(np.resize(levels, k // 32))).repeat(32)
    a = np.empty((k // 512, 16))
    for p in range(k // 512):
        a[p, :8] = np.random.permutation(np.resize(levels, 8))
        for g in range(8):
            far = levels[np.abs(levels - a[p, g]) >= 10]
            a[p, g + 8] = far[np.random.randint(len(far))]
    return np.exp2(a.ravel()).repeat(32)


BF16 = ml_dtypes.bfloat16


def bf(x):
    return np.asarray(x, np.float32).astype(BF16)


def f64(x):
    return np.asarray(x).astype(np.float64)

E4M3FN = np.array([(-1.0 if i & 128 else 1.0) * ((1.0 + (i & 7) / 8.0) * 2.0 ** (((i >> 3) & 15) - 7) if i & 120 else (i & 7) * 2.0 ** -9) for i in range(256)])


def e4m3fn_bytes(y):
    return np.clip(np.asarray(y, np.float64), -448.0, 448.0).astype(np.float32).astype(ml_dtypes.float8_e4m3fn).view(np.uint8)


def e4m3fn_values(b):
    return E4M3FN[b]


M, K, R, B = 4096, 2048, 512, 128

FMAX = 448.0
BETA = 0.9


def setup_inputs():
    s = mx_kscale(K)
    grad = np.random.standard_normal((M, K)) * s
    basis = np.random.standard_normal((R, K)) / np.sqrt(K) / s
    grad_scale = (np.abs(grad).reshape(M, K // B, B).max(axis=2) / FMAX).astype(np.float32)
    basis_scale = (np.abs(basis).reshape(R // B, B, K // B, B).max(axis=(1, 3)) / FMAX).astype(np.float32)
    grad_bytes = e4m3fn_bytes(grad / np.repeat(f64(grad_scale), B, axis=1))
    basis_bytes = e4m3fn_bytes(basis / np.repeat(np.repeat(f64(basis_scale), B, axis=0), B, axis=1))
    return {"grad_bytes": grad_bytes, "grad_scale": grad_scale,
            "basis_bytes": basis_bytes, "basis_scale": basis_scale,
            "mom": bf(np.random.standard_normal((M, R))),
            "lr": bf(0.5 + np.random.random_sample(M))}


def reference(grad_bytes, grad_scale, basis_bytes, basis_scale, mom, lr):
    grad = e4m3fn_values(grad_bytes) * np.repeat(f64(grad_scale), B, axis=1)
    basis = e4m3fn_values(basis_bytes) * np.repeat(np.repeat(f64(basis_scale), B, axis=0), B, axis=1)
    low = mxq(grad, 1, "e4m3") @ mxq(basis, 1, "e4m3").T
    mom_new = BETA * f64(mom) + low
    step = f64(lr)[:, None] * mom_new
    return step, mom_new

@@ -1,0 +1,268 @@
+from contextlib import ExitStack
+
+import concourse.mybir as mybir
+from concourse.masks import make_identity
+
+TOKENS, K, RANK = 4096, 2048, 512
+P = 128
+TILES = TOKENS // P
+PASSES = K // 512
+SCALES = K // 128
+BETA = 0.9
+FLOPS = 2 * TOKENS * K * RANK
+
+F32 = mybir.dt.float32
+BF16 = mybir.dt.bfloat16
+U32 = mybir.dt.uint32
+U8 = mybir.dt.uint8
+FP8 = mybir.dt.float8_e4m3fn
+FP8X4 = mybir.dt.float8_e4m3fn_x4
+MULT = mybir.AluOpType.mult
+ADD = mybir.AluOpType.add
+COPY = mybir.ActivationFunctionType.Copy
+
+V_PASSES = 3
+AHEAD = 5
+
+
+def tile_galore_projected_step_d2_kernel(tc, grad_bytes, grad_scale, basis_bytes, basis_scale, mom, lr, out_0, out_1):
+    nc = tc.nc
+    grad_rows = grad_bytes.rearrange("(p i) k -> p i k", p=P)
+    mom_rows = mom.rearrange("(p i) n -> p i n", p=P)
+    step_rows = out_0.rearrange("(p i) n -> p i n", p=P)
+    new_rows = out_1.rearrange("(p i) n -> p i n", p=P)
+
+    with ExitStack() as ctx:
+        keep = ctx.enter_context(tc.tile_pool(name="keep", bufs=1))
+        load = ctx.enter_context(tc.tile_pool(name="load", bufs=AHEAD + 3))
+        work = ctx.enter_context(tc.tile_pool(name="work", bufs=3))
+        outs = ctx.enter_context(tc.tile_pool(name="outs", bufs=5))
+        psum_t = ctx.enter_context(tc.psum_pool(name="psum_t", bufs=5))
+        psum_m = ctx.enter_context(tc.psum_pool(name="psum_m", bufs=3))
+        ctx.enter_context(tc.manual_schedule())
+
+        ident = keep.tile([P, P], F32, name="ident")
+        make_identity(nc, ident[:])
+
+        basis_sc = keep.tile([P, (RANK // P) * SCALES], F32, name="basis_sc")
+        nc.sync.dma_start(out=basis_sc[:], in_=basis_scale.rearrange("b c -> (b c)").partition_broadcast(P))
+        basis_raw = {}
+        basis_rows = basis_bytes.rearrange("(b p) k -> p b k", p=P)
+        for h in (1, 0):
+            braw = keep.tile([P, RANK // P, K // 2], U8, name="braw%d" % h)
+            nc.sync.dma_start(out=braw[:], in_=basis_rows[:, :, h * (K // 2) : (h + 1) * (K // 2)])
+            basis_raw[h] = braw
+        grad_sc = keep.tile([P, TILES * SCALES], F32, name="grad_sc")
+        nc.sync.dma_start(out=grad_sc[:], in_=grad_scale.rearrange("(p i) c -> p (i c)", p=P))
+
+        graw = {}
+        momt = {}
+
+        def load_grad(m):
+            if m >= TILES // 2:
+                return
+            g = load.tile([P, 2, K], U8, name="g")
+            nc.sync.dma_start(out=g[:], in_=grad_rows[:, 2 * m : 2 * m + 2, :])
+            graw[m] = g
+
+        def load_mom(m):
+            if m >= TILES // 4:
+                return
+            mo = keep.tile([P, 4, RANK], BF16, name="mo%d" % m)
+            nc.sync.dma_start(out=mo[:], in_=mom_rows[:, 4 * m : 4 * m + 4, :])
+            momt[m] = mo
+
+        load_grad(0)
+        lr_raw = keep.tile([P, TILES], BF16, name="lr_raw")
+        nc.sync.dma_start(out=lr_raw[:], in_=lr.rearrange("(p i) -> p i", p=P))
+        load_mom(0)
+        for m in range(1, AHEAD):
+            load_grad(m)
+        load_mom(1)
+
+        dummy = keep.tile([P, 1], F32, name="dummy")
+        nc.scalar.activation(out=dummy[:], in_=ident[:, 0:1], func=COPY)
+
+        def widen_v(dst, src, sc):
+            for q in range(4):
+                nc.vector.tensor_scalar(
+                    out=dst.rearrange("p (u b j) -> p b u j", u=2, j=16)[:, 4 * q : 4 * q + 4],
+                    in0=src[:, 128 * q : 128 * q + 128].bitcast(FP8).rearrange("p (b u j) -> p b u j", u=2, j=16),
+                    scalar1=sc[:, q : q + 1],
+                    scalar2=None,
+                    op0=MULT,
+                )
+
+        def widen_s(dst, src, sc):
+            for q in range(4):
+                nc.scalar.activation(out=dst[:, 128 * q : 128 * q + 128], in_=src[:, 128 * q : 128 * q + 128].bitcast(FP8), func=COPY, scale=sc[:, q : q + 1])
+
+        def words_of(wide, g):
+            w = wide.bitcast(F32)
+            if g < V_PASSES:
+                return w[:, 0:128], w[:, 128:256]
+            return w[:, 0:256:2], w[:, 1:256:2]
+
+        nb = RANK // P
+        bwide = {}
+        for g in range(PASSES):
+            bw = keep.tile([P, nb, 512], BF16, name="bw%d" % g, align_bytes=64)
+            bwide[g] = bw
+        bgroup = {}
+        for g in range(PASSES):
+            bg = keep.tile([P, RANK * 4], BF16, name="bg%d" % g, align_bytes=64)
+            bgroup[g] = bg
+        bcodes = keep.tile([P, PASSES, RANK], U32, name="bcodes", align_bytes=64)
+        bscales = keep.tile([P, PASSES, RANK], U8, name="bscales", align_bytes=64)
+
+        def basis_widen(g):
+            for b in range(nb):
+                src = basis_raw[g // 2][:, b, 512 * (g % 2) : 512 * (g % 2) + 512]
+                sc = basis_sc[:, SCALES * b + 4 * g : SCALES * b + 4 * g + 4]
+                (widen_v if g < V_PASSES else widen_s)(bwide[g][:, b, :], src, sc)
+
+        bbank = {}
+
+        def basis_turn(g):
+            for h in range(2):
+                xt = psum_t.tile([P, 2, 2, P], F32, name="xt")
+                for b in range(2):
+                    for u, w in enumerate(words_of(bwide[g][:, 2 * h + b, :], g)):
+                        nc.tensor.transpose(xt[:, b, u, :], w, ident[:])
+                bbank[g, h] = xt
+
+        def basis_out(g, copy):
+            for h in range(2):
+                copy(
+                    out=bgroup[g][:, 1024 * h : 1024 * h + 1024].bitcast(F32).rearrange("p (b r u) -> p b r u", b=2, u=2),
+                    in_=bbank[g, h][:].rearrange("p b u r -> p b r u"),
+                )
+
+        def basis_quant(g):
+            nc.vector.quantize_mx(out=bcodes[:, g, :].bitcast(FP8X4), scales=bscales[:, g, :], in_=bgroup[g][:])
+
+        wide = {}
+        bank = {}
+        group = {}
+        codes = {}
+        acc = {}
+        new = {}
+        step = {}
+        lr_f = keep.tile([P, TILES], F32, name="lr_f")
+
+        def wv(i):
+            if i >= TILES:
+                return
+            wide_v = work.tile([P, V_PASSES, 512], BF16, name="wide_v", align_bytes=64)
+            for g in range(V_PASSES):
+                widen_v(wide_v[:, g, :], graw[i // 2][:, i % 2, 512 * g : 512 * g + 512], grad_sc[:, SCALES * i + 4 * g : SCALES * i + 4 * g + 4])
+            for g in range(V_PASSES):
+                wide[i, g] = wide_v[:, g, :]
+
+        def ws(i):
+            if i >= TILES:
+                return
+            wide_s = work.tile([P, 512], BF16, name="wide_s", align_bytes=64)
+            g = V_PASSES
+            widen_s(wide_s[:], graw[i // 2][:, i % 2, 512 * g : 512 * g + 512], grad_sc[:, SCALES * i + 4 * g : SCALES * i + 4 * g + 4])
+            wide[i, g] = wide_s[:]
+
+        def turn(i):
+            for h in range(2):
+                xt = psum_t.tile([P, 2, 2, P], F32, name="xt")
+                for gg in range(2):
+                    for u, w in enumerate(words_of(wide[i, 2 * h + gg], 2 * h + gg)):
+                        nc.tensor.transpose(xt[:, gg, u, :], w, ident[:])
+                bank[i, h] = xt
+
+        def out_of_psum(i):
+            grp = work.tile([P, K], BF16, name="grp", align_bytes=64)
+            for h in range(2):
+                nc.scalar.copy(
+                    out=grp[:, 1024 * h : 1024 * h + 1024].bitcast(F32).rearrange("p (g r u) -> p g r u", g=2, u=2),
+                    in_=bank[i, h][:].rearrange("p g u r -> p g r u"),
+                )
+            group[i] = grp
+
+        def quant(i):
+            cod = work.tile([P, PASSES * P], U32, name="cod", align_bytes=64)
+            scl = work.tile([P, PASSES * P], U8, name="scl", align_bytes=64)
+            nc.vector.quantize_mx(out=cod[:].bitcast(FP8X4), scales=scl[:], in_=group[i][:])
+            codes[i] = (cod, scl)
+
+        def mm(i):
+            a = psum_m.tile([P, RANK], F32, name="a")
+            cod, scl = codes[i]
+            for g in range(PASSES):
+                nc.tensor.matmul_mx(
+                    out=a[:],
+                    lhsT=cod[:, P * g : P * g + P].bitcast(FP8X4),
+                    lhsT_scale=scl[:, P * g : P * g + P],
+                    rhs=bcodes[:, g, :].bitcast(FP8X4),
+                    rhs_scale=bscales[:, g, :],
+                    start=(g == 0),
+                    stop=(g == PASSES - 1),
+                )
+            acc[i] = a
+
+        def momentum(i):
+            if i % 2 == 0:
+                nw = outs.tile([P, 2, RANK], F32, name="nw")
+                new[i // 2] = nw
+            nc.vector.scalar_tensor_tensor(
+                out=new[i // 2][:, i % 2, :], in0=momt[i // 4][:, i % 4, :], scalar=BETA, in1=acc[i][:], op0=MULT, op1=ADD)
+
+        def stepped(i):
+            if i % 2 == 0:
+                sp = outs.tile([P, 2, RANK], F32, name="sp")
+                step[i // 2] = sp
+            nc.scalar.activation(out=step[i // 2][:, i % 2, :], in_=new[i // 2][:, i % 2, :], func=COPY, scale=lr_f[:, i : i + 1])
+
+        def store(i):
+            m = i // 2
+            if m == TILES // 2 - 1:
+                nc.sync.dma_start(out=new_rows[:, i, :], in_=new[m][:, i % 2, :])
+                nc.sync.dma_start(out=step_rows[:, i, :], in_=step[m][:, i % 2, :])
+            elif i % 2 == 1:
+                nc.sync.dma_start(out=new_rows[:, 2 * m : 2 * m + 2, :], in_=new[m][:])
+                nc.sync.dma_start(out=step_rows[:, 2 * m : 2 * m + 2, :], in_=step[m][:])
+
+        basis_widen(2)
+        basis_widen(3)
+        basis_turn(2)
+        basis_widen(0)
+        basis_turn(0)
+        basis_out(2, nc.scalar.copy)
+        basis_turn(3)
+        basis_widen(1)
+        basis_turn(1)
+        basis_quant(2)
+        basis_out(0, nc.scalar.copy)
+        basis_out(1, nc.vector.tensor_copy)
+        basis_out(3, nc.scalar.copy)
+        basis_quant(0)
+        ws(0)
+        wv(0)
+        basis_quant(1)
+        basis_quant(3)
+        nc.vector.tensor_copy(out=lr_f[:], in_=lr_raw[:])
+
+        for j in range(TILES + 2):
+            if j % 2 == 0:
+                load_grad(j // 2 + AHEAD)
+            if j % 4 == 2:
+                load_mom(j // 4 + 2)
+            if j < TILES:
+                turn(j)
+                out_of_psum(j)
+            wv(j + 1)
+            ws(j + 1)
+            if j >= 2:
+                momentum(j - 2)
+            if j < TILES:
+                quant(j)
+            if 1 <= j <= TILES:
+                mm(j - 1)
+            if j >= 2:
+                stepped(j - 2)
+                store(j - 2)

@@ -22,7 +22,7 @@ ADD = mybir.AluOpType.add
 COPY = mybir.ActivationFunctionType.Copy
 
 V_PASSES = 3
-AHEAD = 5
+AHEAD = 8
 
 
 def tile_galore_projected_step_d2_kernel(tc, grad_bytes, grad_scale, basis_bytes, basis_scale, mom, lr, out_0, out_1):
@@ -205,24 +205,30 @@ def tile_galore_projected_step_d2_kernel(tc, grad_bytes, grad_scale, basis_bytes
                 )
             acc[i] = a
 
+        def halves(i):
+            return [slice(0, 256), slice(256, 512)] if i == TILES - 1 else [slice(0, 512)]
+
         def momentum(i):
             if i % 2 == 0:
                 nw = outs.tile([P, 2, RANK], F32, name="nw")
                 new[i // 2] = nw
-            nc.vector.scalar_tensor_tensor(
-                out=new[i // 2][:, i % 2, :], in0=momt[i // 4][:, i % 4, :], scalar=BETA, in1=acc[i][:], op0=MULT, op1=ADD)
+            for c in halves(i):
+                nc.vector.scalar_tensor_tensor(
+                    out=new[i // 2][:, i % 2, c], in0=momt[i // 4][:, i % 4, c], scalar=BETA, in1=acc[i][:, c], op0=MULT, op1=ADD)
 
         def stepped(i):
             if i % 2 == 0:
                 sp = outs.tile([P, 2, RANK], F32, name="sp")
                 step[i // 2] = sp
-            nc.scalar.activation(out=step[i // 2][:, i % 2, :], in_=new[i // 2][:, i % 2, :], func=COPY, scale=lr_f[:, i : i + 1])
+            for c in halves(i):
+                nc.scalar.activation(out=step[i // 2][:, i % 2, c], in_=new[i // 2][:, i % 2, c], func=COPY, scale=lr_f[:, i : i + 1])
 
         def store(i):
             m = i // 2
             if m == TILES // 2 - 1:
-                nc.sync.dma_start(out=new_rows[:, i, :], in_=new[m][:, i % 2, :])
-                nc.sync.dma_start(out=step_rows[:, i, :], in_=step[m][:, i % 2, :])
+                for c in halves(i):
+                    nc.sync.dma_start(out=new_rows[:, i, c], in_=new[m][:, i % 2, c])
+                    nc.sync.dma_start(out=step_rows[:, i, c], in_=step[m][:, i % 2, c])
             elif i % 2 == 1:
                 nc.sync.dma_start(out=new_rows[:, 2 * m : 2 * m + 2, :], in_=new[m][:])
                 nc.sync.dma_start(out=step_rows[:, 2 * m : 2 * m + 2, :], in_=step[m][:])
@@ -240,29 +246,33 @@ def tile_galore_projected_step_d2_kernel(tc, grad_bytes, grad_scale, basis_bytes
         basis_out(0, nc.scalar.copy)
         basis_out(1, nc.vector.tensor_copy)
         basis_out(3, nc.scalar.copy)
-        basis_quant(0)
         ws(0)
         wv(0)
+        basis_quant(0)
+        turn(0)
         basis_quant(1)
+        ws(1)
+        wv(1)
         basis_quant(3)
         nc.vector.tensor_copy(out=lr_f[:], in_=lr_raw[:])
 
-        for j in range(TILES + 2):
+        for j in range(TILES + 3):
             if j % 2 == 0:
                 load_grad(j // 2 + AHEAD)
             if j % 4 == 2:
                 load_mom(j // 4 + 2)
             if j < TILES:
-                turn(j)
                 out_of_psum(j)
-            wv(j + 1)
-            ws(j + 1)
-            if j >= 2:
+            wv(j + 2)
+            ws(j + 2)
+            if j + 1 < TILES:
+                turn(j + 1)
+            if 2 <= j < TILES + 2:
                 momentum(j - 2)
             if j < TILES:
                 quant(j)
             if 1 <= j <= TILES:
                 mm(j - 1)
-            if j >= 2:
-                stepped(j - 2)
-                store(j - 2)
+            if j >= 3:
+                stepped(j - 3)
+                store(j - 3)

from contextlib import ExitStack

import concourse.mybir as mybir
from concourse.masks import make_identity

TOKENS, K, RANK = 4096, 2048, 512
P = 128
TILES = TOKENS // P
PASSES = K // 512
SCALES = K // 128
BETA = 0.9
FLOPS = 2 * TOKENS * K * RANK

F32 = mybir.dt.float32
BF16 = mybir.dt.bfloat16
U32 = mybir.dt.uint32
U8 = mybir.dt.uint8
FP8 = mybir.dt.float8_e4m3fn
FP8X4 = mybir.dt.float8_e4m3fn_x4
MULT = mybir.AluOpType.mult
ADD = mybir.AluOpType.add
COPY = mybir.ActivationFunctionType.Copy

V_PASSES = 3
AHEAD = 8


def tile_galore_projected_step_d2_kernel(tc, grad_bytes, grad_scale, basis_bytes, basis_scale, mom, lr, out_0, out_1):
    nc = tc.nc
    grad_rows = grad_bytes.rearrange("(p i) k -> p i k", p=P)
    mom_rows = mom.rearrange("(p i) n -> p i n", p=P)
    step_rows = out_0.rearrange("(p i) n -> p i n", p=P)
    new_rows = out_1.rearrange("(p i) n -> p i n", p=P)

    with ExitStack() as ctx:
        keep = ctx.enter_context(tc.tile_pool(name="keep", bufs=1))
        load = ctx.enter_context(tc.tile_pool(name="load", bufs=AHEAD + 3))
        work = ctx.enter_context(tc.tile_pool(name="work", bufs=3))
        outs = ctx.enter_context(tc.tile_pool(name="outs", bufs=5))
        psum_t = ctx.enter_context(tc.psum_pool(name="psum_t", bufs=5))
        psum_m = ctx.enter_context(tc.psum_pool(name="psum_m", bufs=3))
        ctx.enter_context(tc.manual_schedule())

        ident = keep.tile([P, P], F32, name="ident")
        make_identity(nc, ident[:])

        basis_sc = keep.tile([P, (RANK // P) * SCALES], F32, name="basis_sc")
        nc.sync.dma_start(out=basis_sc[:], in_=basis_scale.rearrange("b c -> (b c)").partition_broadcast(P))
        basis_raw = {}
        basis_rows = basis_bytes.rearrange("(b p) k -> p b k", p=P)
        for h in (1, 0):
            braw = keep.tile([P, RANK // P, K // 2], U8, name="braw%d" % h)
            nc.sync.dma_start(out=braw[:], in_=basis_rows[:, :, h * (K // 2) : (h + 1) * (K // 2)])
            basis_raw[h] = braw
        grad_sc = keep.tile([P, TILES * SCALES], F32, name="grad_sc")
        nc.sync.dma_start(out=grad_sc[:], in_=grad_scale.rearrange("(p i) c -> p (i c)", p=P))

        graw = {}
        momt = {}

        def load_grad(m):
            if m >= TILES // 2:
                return
            g = load.tile([P, 2, K], U8, name="g")
            nc.sync.dma_start(out=g[:], in_=grad_rows[:, 2 * m : 2 * m + 2, :])
            graw[m] = g

        def load_mom(m):
            if m >= TILES // 4:
                return
            mo = keep.tile([P, 4, RANK], BF16, name="mo%d" % m)
            nc.sync.dma_start(out=mo[:], in_=mom_rows[:, 4 * m : 4 * m + 4, :])
            momt[m] = mo

        load_grad(0)
        lr_raw = keep.tile([P, TILES], BF16, name="lr_raw")
        nc.sync.dma_start(out=lr_raw[:], in_=lr.rearrange("(p i) -> p i", p=P))
        load_mom(0)
        for m in range(1, AHEAD):
            load_grad(m)
        load_mom(1)

        dummy = keep.tile([P, 1], F32, name="dummy")
        nc.scalar.activation(out=dummy[:], in_=ident[:, 0:1], func=COPY)

        def widen_v(dst, src, sc):
            for q in range(4):
                nc.vector.tensor_scalar(
                    out=dst.rearrange("p (u b j) -> p b u j", u=2, j=16)[:, 4 * q : 4 * q + 4],
                    in0=src[:, 128 * q : 128 * q + 128].bitcast(FP8).rearrange("p (b u j) -> p b u j", u=2, j=16),
                    scalar1=sc[:, q : q + 1],
                    scalar2=None,
                    op0=MULT,
                )

        def widen_s(dst, src, sc):
            for q in range(4):
                nc.scalar.activation(out=dst[:, 128 * q : 128 * q + 128], in_=src[:, 128 * q : 128 * q + 128].bitcast(FP8), func=COPY, scale=sc[:, q : q + 1])

        def words_of(wide, g):
            w = wide.bitcast(F32)
            if g < V_PASSES:
                return w[:, 0:128], w[:, 128:256]
            return w[:, 0:256:2], w[:, 1:256:2]

        nb = RANK // P
        bwide = {}
        for g in range(PASSES):
            bw = keep.tile([P, nb, 512], BF16, name="bw%d" % g, align_bytes=64)
            bwide[g] = bw
        bgroup = {}
        for g in range(PASSES):
            bg = keep.tile([P, RANK * 4], BF16, name="bg%d" % g, align_bytes=64)
            bgroup[g] = bg
        bcodes = keep.tile([P, PASSES, RANK], U32, name="bcodes", align_bytes=64)
        bscales = keep.tile([P, PASSES, RANK], U8, name="bscales", align_bytes=64)

        def basis_widen(g):
            for b in range(nb):
                src = basis_raw[g // 2][:, b, 512 * (g % 2) : 512 * (g % 2) + 512]
                sc = basis_sc[:, SCALES * b + 4 * g : SCALES * b + 4 * g + 4]
                (widen_v if g < V_PASSES else widen_s)(bwide[g][:, b, :], src, sc)

        bbank = {}

        def basis_turn(g):
            for h in range(2):
                xt = psum_t.tile([P, 2, 2, P], F32, name="xt")
                for b in range(2):
                    for u, w in enumerate(words_of(bwide[g][:, 2 * h + b, :], g)):
                        nc.tensor.transpose(xt[:, b, u, :], w, ident[:])
                bbank[g, h] = xt

        def basis_out(g, copy):
            for h in range(2):
                copy(
                    out=bgroup[g][:, 1024 * h : 1024 * h + 1024].bitcast(F32).rearrange("p (b r u) -> p b r u", b=2, u=2),
                    in_=bbank[g, h][:].rearrange("p b u r -> p b r u"),
                )

        def basis_quant(g):
            nc.vector.quantize_mx(out=bcodes[:, g, :].bitcast(FP8X4), scales=bscales[:, g, :], in_=bgroup[g][:])

        wide = {}
        bank = {}
        group = {}
        codes = {}
        acc = {}
        new = {}
        step = {}
        lr_f = keep.tile([P, TILES], F32, name="lr_f")

        def wv(i):
            if i >= TILES:
                return
            wide_v = work.tile([P, V_PASSES, 512], BF16, name="wide_v", align_bytes=64)
            for g in range(V_PASSES):
                widen_v(wide_v[:, g, :], graw[i // 2][:, i % 2, 512 * g : 512 * g + 512], grad_sc[:, SCALES * i + 4 * g : SCALES * i + 4 * g + 4])
            for g in range(V_PASSES):
                wide[i, g] = wide_v[:, g, :]

        def ws(i):
            if i >= TILES:
                return
            wide_s = work.tile([P, 512], BF16, name="wide_s", align_bytes=64)
            g = V_PASSES
            widen_s(wide_s[:], graw[i // 2][:, i % 2, 512 * g : 512 * g + 512], grad_sc[:, SCALES * i + 4 * g : SCALES * i + 4 * g + 4])
            wide[i, g] = wide_s[:]

        def turn(i):
            for h in range(2):
                xt = psum_t.tile([P, 2, 2, P], F32, name="xt")
                for gg in range(2):
                    for u, w in enumerate(words_of(wide[i, 2 * h + gg], 2 * h + gg)):
                        nc.tensor.transpose(xt[:, gg, u, :], w, ident[:])
                bank[i, h] = xt

        def out_of_psum(i):
            grp = work.tile([P, K], BF16, name="grp", align_bytes=64)
            for h in range(2):
                nc.scalar.copy(
                    out=grp[:, 1024 * h : 1024 * h + 1024].bitcast(F32).rearrange("p (g r u) -> p g r u", g=2, u=2),
                    in_=bank[i, h][:].rearrange("p g u r -> p g r u"),
                )
            group[i] = grp

        def quant(i):
            cod = work.tile([P, PASSES * P], U32, name="cod", align_bytes=64)
            scl = work.tile([P, PASSES * P], U8, name="scl", align_bytes=64)
            nc.vector.quantize_mx(out=cod[:].bitcast(FP8X4), scales=scl[:], in_=group[i][:])
            codes[i] = (cod, scl)

        def mm(i):
            a = psum_m.tile([P, RANK], F32, name="a")
            cod, scl = codes[i]
            for g in range(PASSES):
                nc.tensor.matmul_mx(
                    out=a[:],
                    lhsT=cod[:, P * g : P * g + P].bitcast(FP8X4),
                    lhsT_scale=scl[:, P * g : P * g + P],
                    rhs=bcodes[:, g, :].bitcast(FP8X4),
                    rhs_scale=bscales[:, g, :],
                    start=(g == 0),
                    stop=(g == PASSES - 1),
                )
            acc[i] = a

        def halves(i):
            return [slice(0, 256), slice(256, 512)] if i == TILES - 1 else [slice(0, 512)]

        def momentum(i):
            if i % 2 == 0:
                nw = outs.tile([P, 2, RANK], F32, name="nw")
                new[i // 2] = nw
            for c in halves(i):
                nc.vector.scalar_tensor_tensor(
                    out=new[i // 2][:, i % 2, c], in0=momt[i // 4][:, i % 4, c], scalar=BETA, in1=acc[i][:, c], op0=MULT, op1=ADD)

        def stepped(i):
            if i % 2 == 0:
                sp = outs.tile([P, 2, RANK], F32, name="sp")
                step[i // 2] = sp
            for c in halves(i):
                nc.scalar.activation(out=step[i // 2][:, i % 2, c], in_=new[i // 2][:, i % 2, c], func=COPY, scale=lr_f[:, i : i + 1])

        def store(i):
            m = i // 2
            if m == TILES // 2 - 1:
                for c in halves(i):
                    nc.sync.dma_start(out=new_rows[:, i, c], in_=new[m][:, i % 2, c])
                    nc.sync.dma_start(out=step_rows[:, i, c], in_=step[m][:, i % 2, c])
            elif i % 2 == 1:
                nc.sync.dma_start(out=new_rows[:, 2 * m : 2 * m + 2, :], in_=new[m][:])
                nc.sync.dma_start(out=step_rows[:, 2 * m : 2 * m + 2, :], in_=step[m][:])

        basis_widen(2)
        basis_widen(3)
        basis_turn(2)
        basis_widen(0)
        basis_turn(0)
        basis_out(2, nc.scalar.copy)
        basis_turn(3)
        basis_widen(1)
        basis_turn(1)
        basis_quant(2)
        basis_out(0, nc.scalar.copy)
        basis_out(1, nc.vector.tensor_copy)
        basis_out(3, nc.scalar.copy)
        ws(0)
        wv(0)
        basis_quant(0)
        turn(0)
        basis_quant(1)
        ws(1)
        wv(1)
        basis_quant(3)
        nc.vector.tensor_copy(out=lr_f[:], in_=lr_raw[:])

        for j in range(TILES + 3):
            if j % 2 == 0:
                load_grad(j // 2 + AHEAD)
            if j % 4 == 2:
                load_mom(j // 4 + 2)
            if j < TILES:
                out_of_psum(j)
            wv(j + 2)
            ws(j + 2)
            if j + 1 < TILES:
                turn(j + 1)
            if 2 <= j < TILES + 2:
                momentum(j - 2)
            if j < TILES:
                quant(j)
            if 1 <= j <= TILES:
                mm(j - 1)
            if j >= 3:
                stepped(j - 3)
                store(j - 3)
